import numpy as np
import ml_dtypes


def mxq(x, axis, fmt="e4m3"):
    dtype, down = {"e4m3": (ml_dtypes.float8_e4m3fn, 7), "e5m2": (ml_dtypes.float8_e5m2, 14)}[fmt]
    v = np.moveaxis(np.asarray(x, np.float32).astype(ml_dtypes.bfloat16).astype(np.float64), axis, -1)
    blocks = v.reshape(v.shape[:-1] + (-1, 32))
    amax = np.abs(blocks).max(-1, keepdims=True)
    byte = np.maximum(np.where(amax > 0, np.frexp(amax)[1] - 1 + 127, 0) - down, 1)
    scale = np.exp2(byte - 127.0)
    codes = (blocks / scale).astype(np.float32).astype(dtype).astype(np.float64)
    return np.moveaxis((codes * scale).reshape(v.shape), -1, axis)


WIDE = False


def mx_kscale(k):
    if not WIDE:
        return np.ones(k)
    levels = np.array([10, -10, 5, -5, 0])
    if k % 512:
        return np.exp2(np.random.permutation(np.resize(levels, k // 32))).repeat(32)
    a = np.empty((k // 512, 16))
    for p in range(k // 512):
        a[p, :8] = np.random.permutation(np.resize(levels, 8))
        for g in range(8):
            far = levels[np.abs(levels - a[p, g]) >= 10]
            a[p, g + 8] = far[np.random.randint(len(far))]
    return np.exp2(a.ravel()).repeat(32)


def f64(x):
    return np.asarray(x).astype(np.float64)


def striped(idx):
    return np.tile(idx.reshape(-1, 16).T, (8, 1)).astype(np.uint16)


def unstriped(offs):
    return offs[:16].T.reshape(-1).astype(np.int64)


def gelu(v):
    return 0.5 * v * (1.0 + np.tanh(np.sqrt(2.0 / np.pi) * (v + 0.044715 * v**3)))


K, T, S, H, N, U = 512, 2048, 512, 512, 256, 1024


def setup_inputs():
    n = np.random.standard_normal
    s = mx_kscale(K)[:, None]
    u = mx_kscale(H)
    return {
        "xT": (n((K, T)) * s).astype(np.float32),
        "w1": (n((K, H)) / np.sqrt(K) / s * u).astype(np.float32),
        "w2": (n((H, N)) / np.sqrt(H) / u[:, None]).astype(np.float32),
        "skip": (n((H, U)) * u[:, None]).astype(np.float32),
        "offs": striped(np.random.permutation(T)[:S]),
        "cell": striped(np.random.permutation(U)[:S]),
    }


def reference(xT, w1, w2, skip, offs, cell):
    xq = mxq(f64(xT)[:, unstriped(offs)], 0, "e4m3")
    up = np.zeros((H, U))
    up[:, unstriped(cell)] = gelu(mxq(f64(w1), 0, "e4m3").T @ xq)
    z = up + f64(skip)
    return mxq(f64(w2), 0, "e4m3").T @ mxq(z, 0, "e4m3")

@@ -1,0 +1,182 @@
+from contextlib import ExitStack
+
+import concourse.mybir as mybir
+
+K, T, S, H, N, U = 512, 2048, 512, 512, 256, 1024
+FLOPS = 2 * K * H * S + 2 * H * N * U
+
+F32 = mybir.dt.float32
+BF16 = mybir.dt.bfloat16
+U32 = mybir.dt.uint32
+U16 = mybir.dt.uint16
+U8 = mybir.dt.uint8
+FP8X4 = mybir.dt.float8_e4m3fn_x4
+ADD = mybir.AluOpType.add
+GELU = mybir.ActivationFunctionType.Gelu_apprx_tanh
+
+P = 128
+PACK = 4
+HALF = S // 2
+LANES = 16
+CELLS = 256
+CHUNKS = U // CELLS
+W1_HALF = H // 2
+M_HALF = W1_HALF // PACK
+
+
+def quantise(nc, words, scales, grouped):
+    nc.vector.quantize_mx(out=words.bitcast(FP8X4), scales=scales, in_=grouped)
+
+
+def product(nc, bank, w_words, w_scales, a_words, a_scales):
+    nc.tensor.matmul_mx(
+        out=bank,
+        lhsT=w_words.bitcast(FP8X4),
+        lhsT_scale=w_scales,
+        rhs=a_words.bitcast(FP8X4),
+        rhs_scale=a_scales,
+        start=True,
+        stop=True,
+    )
+
+
+def tile_picked_unet_gelu_e_kernel(tc, xT, w1, w2, skip, offs, cell, out):
+    nc = tc.nc
+    with ExitStack() as ctx:
+        lists = ctx.enter_context(tc.tile_pool(name="lists", bufs=1))
+        keep = ctx.enter_context(tc.tile_pool(name="keep", bufs=1))
+        psum = ctx.enter_context(tc.psum_pool(name="psum", bufs=8))
+
+        offs_sb = lists.tile([P, S // LANES], U16, name="offs_sb")
+        cell_sb = lists.tile([P, S // LANES], U16, name="cell_sb")
+        x_rows = [keep.tile([P, T], F32, name=f"x_rows{j}") for j in range(PACK)]
+        w1_raw = [keep.tile([P, PACK, W1_HALF], F32, name=f"w1_raw{u}") for u in range(2)]
+        w2_raw = keep.tile([P, PACK, N], F32, name="w2_raw")
+        skip_rows = [keep.tile([P, U], F32, name=f"skip_rows{t}") for t in range(PACK)]
+
+        x_view = xT.rearrange("(p j) c -> p j c", j=PACK)
+        w1_view = w1.rearrange("(p j) c -> p j c", j=PACK)
+        skip_view = skip.rearrange("(p t) v -> p t v", t=PACK)
+        nc.sync.dma_start(offs_sb[:], offs)
+        for j in range(PACK):
+            nc.sync.dma_start(x_rows[j][:], x_view[:, j, :])
+        for u in range(2):
+            nc.sync.dma_start(w1_raw[u][:], w1_view[:, :, u * W1_HALF : (u + 1) * W1_HALF])
+        nc.sync.dma_start(cell_sb[:], cell)
+        nc.sync.dma_start(w2_raw[:], w2.rearrange("(p j) c -> p j c", j=PACK))
+        for t in range(PACK):
+            nc.sync.dma_start(skip_rows[t][:], skip_view[:, t, :])
+
+        up = [keep.tile([P, U], F32, name=f"up{t}") for t in range(PACK)]
+        for t in range(PACK):
+            nc.vector.memset(up[t][:], 0.0)
+        warm_in = keep.tile([P, 8], F32, name="warm_in")
+        warm_out = keep.tile([P, 8], F32, name="warm_out")
+        nc.vector.memset(warm_in[:], 0.0)
+        nc.scalar.activation(warm_out[:], warm_in[:], GELU)
+
+        x_grouped = keep.tile([P, S, PACK], BF16, name="x_grouped", align_bytes=64)
+        x_words = keep.tile([P, S], U32, name="x_words", align_bytes=64)
+        x_scales = keep.tile([P, S], U8, name="x_scales", align_bytes=64)
+        halves = [slice(h * HALF, (h + 1) * HALF) for h in range(2)]
+        list_halves = [slice(h * HALF // LANES, (h + 1) * HALF // LANES) for h in range(2)]
+        for j in range(PACK - 1):
+            nc.vector.tensor_copy(x_grouped[:, :, j], x_rows[j][:].indirect(offs_sb[:]))
+        for h in range(2):
+            nc.vector.tensor_copy(x_grouped[:, halves[h], PACK - 1], x_rows[PACK - 1][:].indirect(offs_sb[:, list_halves[h]]))
+        for h in range(2):
+            quantise(nc, x_words[:, halves[h]], x_scales[:, halves[h]], x_grouped[:, halves[h], :].rearrange("p s j -> p (s j)"))
+
+        w1_first = keep.tile([P, P, PACK], BF16, name="w1_first", align_bytes=64)
+        w1_rest = keep.tile([P, PACK - 1, P, PACK], BF16, name="w1_rest", align_bytes=64)
+        w1_words = [keep.tile([P, P], U32, name=f"w1_words{t}", align_bytes=64) for t in range(PACK)]
+        w1_scales = [keep.tile([P, P], U8, name=f"w1_scales{t}", align_bytes=64) for t in range(PACK)]
+
+        def deal_w1(copy, u, first):
+            dealt = w1_raw[u][:].rearrange("p j (m t) -> p m j t", t=PACK)
+            ms = slice(u * M_HALF, (u + 1) * M_HALF)
+            if first:
+                copy(w1_first[:, ms, :], dealt[:, :, :, 0])
+            else:
+                copy(w1_rest[:, :, ms, :].rearrange("p t m j -> p m j t"), dealt[:, :, :, 1:PACK])
+
+        deal_w1(nc.scalar.copy, 0, True)
+        deal_w1(nc.scalar.copy, 0, False)
+        deal_w1(nc.vector.tensor_copy, 1, True)
+        quantise(nc, w1_words[0][:], w1_scales[0][:], w1_first[:].rearrange("p m j -> p (m j)"))
+        deal_w1(nc.vector.tensor_copy, 1, False)
+        for t in range(1, PACK):
+            quantise(nc, w1_words[t][:], w1_scales[t][:], w1_rest[:, t - 1, :, :].rearrange("p m j -> p (m j)"))
+
+        z_planes = keep.tile([P, CHUNKS, PACK, CELLS], BF16, name="z_planes")
+        whole, whole_list = slice(0, S), slice(0, S // LANES)
+        pieces = [(0, halves[0], list_halves[0]), (1, halves[0], list_halves[0]), (0, halves[1], list_halves[1]), (1, halves[1], list_halves[1]), (2, whole, whole_list), (3, whole, whole_list)]
+        for n, (t, entries, columns) in enumerate(pieces):
+            width = entries.stop - entries.start
+            bank = psum.tile([P, S], F32, name="bank")
+            product(nc, bank[:, 0:width], w1_words[t][:], w1_scales[t][:], x_words[:, entries], x_scales[:, entries])
+            hidden = keep.tile([P, width], F32, name=f"hidden{n}")
+            nc.scalar.activation(hidden[:], bank[:, 0:width], GELU)
+            nc.vector.tensor_copy(up[t][:].indirect(cell_sb[:, columns]), hidden[:])
+            if entries.stop == S and t < PACK - 1:
+                nc.gpsimd.tensor_tensor(
+                    z_planes[:, :, t, :],
+                    up[t][:].rearrange("p (c v) -> p c v", v=CELLS),
+                    skip_rows[t][:].rearrange("p (c v) -> p c v", v=CELLS),
+                    ADD,
+                )
+
+        w2_grouped = keep.tile([P, N, PACK], BF16, name="w2_grouped", align_bytes=64)
+        w2_words = keep.tile([P, N], U32, name="w2_words", align_bytes=64)
+        w2_scales = keep.tile([P, N], U8, name="w2_scales", align_bytes=64)
+        nc.scalar.copy(
+            w2_grouped[:].rearrange("p (c i) j -> p c j i", i=4),
+            w2_raw[:].rearrange("p j (c i) -> p c j i", i=4),
+        )
+        quantise(nc, w2_words[:], w2_scales[:], w2_grouped[:].rearrange("p m j -> p (m j)"))
+
+        z_grouped = [keep.tile([P, CELLS, PACK], BF16, name=f"z_grouped{c}", align_bytes=64) for c in range(CHUNKS)]
+        z_words = [keep.tile([P, CELLS], U32, name=f"z_words{c}", align_bytes=64) for c in range(CHUNKS)]
+        z_scales = [keep.tile([P, CELLS], U8, name=f"z_scales{c}", align_bytes=64) for c in range(CHUNKS)]
+        result = [keep.tile([P, N // P, CELLS], F32, name=f"result{c}") for c in range(CHUNKS)]
+        out_view = out.rearrange("(b p) v -> p b v", p=P)
+        last = PACK - 1
+
+        def add_last(c):
+            cells = slice(c * CELLS, (c + 1) * CELLS)
+            nc.vector.tensor_tensor(z_planes[:, c, last, :], up[last][:, cells], skip_rows[last][:, cells], ADD)
+
+        def weave(copy, c):
+            copy(
+                z_grouped[c][:].rearrange("p (g i) t -> p g t i", i=4),
+                z_planes[:, c, :, :].rearrange("p t (g i) -> p g t i", i=4),
+            )
+
+        def quantise_z(c):
+            quantise(nc, z_words[c][:], z_scales[c][:], z_grouped[c][:].rearrange("p v t -> p (v t)"))
+
+        def finish(c, copies):
+            for b in range(N // P):
+                bank = psum.tile([P, S], F32, name="bank")
+                rows = slice(b * P, (b + 1) * P)
+                product(nc, bank[:, 0:CELLS], w2_words[:, rows], w2_scales[:, rows], z_words[c][:], z_scales[c][:])
+                copies[b](result[c][:, b, :], bank[:, 0:CELLS])
+            nc.sync.dma_start(out_view[:, :, c * CELLS : (c + 1) * CELLS], result[c][:])
+
+        on_scalar, on_vector = nc.scalar.copy, nc.vector.tensor_copy
+        add_last(0)
+        weave(on_scalar, 0)
+        add_last(3)
+        weave(on_scalar, 3)
+        add_last(1)
+        add_last(2)
+        weave(on_vector, 1)
+        quantise_z(0)
+        finish(0, [on_scalar, on_scalar])
+        quantise_z(1)
+        finish(1, [on_scalar, on_scalar])
+        weave(on_vector, 2)
+        quantise_z(3)
+        finish(3, [on_scalar, on_vector])
+        quantise_z(2)
+        finish(2, [on_scalar, on_vector])

@@ -1,6 +1,7 @@
 from contextlib import ExitStack
 
 import concourse.mybir as mybir
+from concourse.masks import make_identity
 
 K, T, S, H, N, U = 512, 2048, 512, 512, 256, 1024
 FLOPS = 2 * K * H * S + 2 * H * N * U
@@ -22,6 +23,8 @@ CELLS = 256
 CHUNKS = U // CELLS
 W1_HALF = H // 2
 M_HALF = W1_HALF // PACK
+ORDER = (0, 2, 3, 1)
+BLOCKS = CELLS // P
 
 
 def quantise(nc, words, scales, grouped):
@@ -63,8 +66,9 @@ def tile_picked_unet_gelu_e_kernel(tc, xT, w1, w2, skip, offs, cell, out):
         for u in range(2):
             nc.sync.dma_start(w1_raw[u][:], w1_view[:, :, u * W1_HALF : (u + 1) * W1_HALF])
         nc.sync.dma_start(cell_sb[:], cell)
+        nc.sync.dma_start(skip_rows[ORDER[0]][:], skip_view[:, ORDER[0], :])
         nc.sync.dma_start(w2_raw[:], w2.rearrange("(p j) c -> p j c", j=PACK))
-        for t in range(PACK):
+        for t in ORDER[1:]:
             nc.sync.dma_start(skip_rows[t][:], skip_view[:, t, :])
 
         up = [keep.tile([P, U], F32, name=f"up{t}") for t in range(PACK)]
@@ -105,12 +109,24 @@ def tile_picked_unet_gelu_e_kernel(tc, xT, w1, w2, skip, offs, cell, out):
         deal_w1(nc.vector.tensor_copy, 1, True)
         quantise(nc, w1_words[0][:], w1_scales[0][:], w1_first[:].rearrange("p m j -> p (m j)"))
         deal_w1(nc.vector.tensor_copy, 1, False)
-        for t in range(1, PACK):
+        for t in ORDER[1:]:
             quantise(nc, w1_words[t][:], w1_scales[t][:], w1_rest[:, t - 1, :, :].rearrange("p m j -> p (m j)"))
 
-        z_planes = keep.tile([P, CHUNKS, PACK, CELLS], BF16, name="z_planes")
+        eye32 = keep.tile([P, P], F32, name="eye32")
+        eye16 = keep.tile([P, P], BF16, name="eye16")
+        make_identity(nc, eye32[:])
+        make_identity(nc, eye16[:])
+
+        first, second, third, last = ORDER
         whole, whole_list = slice(0, S), slice(0, S // LANES)
-        pieces = [(0, halves[0], list_halves[0]), (1, halves[0], list_halves[0]), (0, halves[1], list_halves[1]), (1, halves[1], list_halves[1]), (2, whole, whole_list), (3, whole, whole_list)]
+        pieces = [
+            (first, halves[0], list_halves[0]),
+            (second, halves[0], list_halves[0]),
+            (first, halves[1], list_halves[1]),
+            (second, halves[1], list_halves[1]),
+            (third, whole, whole_list),
+            (last, whole, whole_list),
+        ]
         for n, (t, entries, columns) in enumerate(pieces):
             width = entries.stop - entries.start
             bank = psum.tile([P, S], F32, name="bank")
@@ -118,13 +134,6 @@ def tile_picked_unet_gelu_e_kernel(tc, xT, w1, w2, skip, offs, cell, out):
             hidden = keep.tile([P, width], F32, name=f"hidden{n}")
             nc.scalar.activation(hidden[:], bank[:, 0:width], GELU)
             nc.vector.tensor_copy(up[t][:].indirect(cell_sb[:, columns]), hidden[:])
-            if entries.stop == S and t < PACK - 1:
-                nc.gpsimd.tensor_tensor(
-                    z_planes[:, :, t, :],
-                    up[t][:].rearrange("p (c v) -> p c v", v=CELLS),
-                    skip_rows[t][:].rearrange("p (c v) -> p c v", v=CELLS),
-                    ADD,
-                )
 
         w2_grouped = keep.tile([P, N, PACK], BF16, name="w2_grouped", align_bytes=64)
         w2_words = keep.tile([P, N], U32, name="w2_words", align_bytes=64)
@@ -135,21 +144,61 @@ def tile_picked_unet_gelu_e_kernel(tc, xT, w1, w2, skip, offs, cell, out):
         )
         quantise(nc, w2_words[:], w2_scales[:], w2_grouped[:].rearrange("p m j -> p (m j)"))
 
+        def summed_and_turned(t):
+            sums = [psum.tile([P, 4, P], F32, name="bank") for g in range(2)]
+            for source, start, stop in ((skip_rows[t], True, False), (up[t], False, True)):
+                for block in range(U // P):
+                    g, q = divmod(block, 4)
+                    nc.tensor.matmul(
+                        sums[g][:, q, :],
+                        source[:, block * P : (block + 1) * P],
+                        eye32[:],
+                        start=start and q == 0,
+                        stop=stop and q == 3,
+                        is_transpose=True,
+                    )
+            return sums
+
+        pairs = [keep.tile([P, 2, CELLS, 2], BF16, name=f"pairs{c}") for c in range(CHUNKS)]
+
+        lone_sums = summed_and_turned(first)
+        lone_back = psum.tile([P, U], BF16, name="bank")
+        for g in range(2):
+            lone_turned = keep.tile([P, 4, P], BF16, name=f"lone_turned{g}")
+            nc.scalar.copy(lone_turned[:], lone_sums[g][:])
+            for q in range(4):
+                block = 4 * g + q
+                nc.tensor.transpose(lone_back[:, block * P : (block + 1) * P], lone_turned[:, q, :], eye16[:])
+        for c in range(CHUNKS):
+            nc.scalar.copy(pairs[c][:, 0, :, :], lone_back[:, c * CELLS : (c + 1) * CELLS].unsqueeze(2).to_broadcast([P, CELLS, 2]))
+
+        pair_turned = [keep.tile([P, 4 * P, 2], BF16, name=f"pair_turned{g}") for g in range(2)]
+        for e, t in enumerate((second, third)):
+            sums = summed_and_turned(t)
+            for g in range(2):
+                nc.scalar.copy(pair_turned[g][:, :, e], sums[g][:].rearrange("p q m -> p (q m)"))
+        for c in range(CHUNKS):
+            g, place = divmod(c * CELLS, 4 * P)
+            words = pair_turned[g][:].rearrange("p w e -> p (w e)").bitcast(F32)
+            pair_back = psum.tile([P, CELLS], F32, name="bank")
+            for q in range(BLOCKS):
+                nc.tensor.transpose(pair_back[:, q * P : (q + 1) * P], words[:, place + q * P : place + (q + 1) * P], eye32[:])
+            nc.scalar.copy(pairs[c][:, 1, :, :].rearrange("p v e -> p (v e)").bitcast(F32), pair_back[:])
+
         z_grouped = [keep.tile([P, CELLS, PACK], BF16, name=f"z_grouped{c}", align_bytes=64) for c in range(CHUNKS)]
         z_words = [keep.tile([P, CELLS], U32, name=f"z_words{c}", align_bytes=64) for c in range(CHUNKS)]
         z_scales = [keep.tile([P, CELLS], U8, name=f"z_scales{c}", align_bytes=64) for c in range(CHUNKS)]
         result = [keep.tile([P, N // P, CELLS], F32, name=f"result{c}") for c in range(CHUNKS)]
         out_view = out.rearrange("(b p) v -> p b v", p=P)
-        last = PACK - 1
 
         def add_last(c):
             cells = slice(c * CELLS, (c + 1) * CELLS)
-            nc.vector.tensor_tensor(z_planes[:, c, last, :], up[last][:, cells], skip_rows[last][:, cells], ADD)
+            nc.vector.tensor_tensor(pairs[c][:, 0, :, 1], up[last][:, cells], skip_rows[last][:, cells], ADD)
 
         def weave(copy, c):
             copy(
-                z_grouped[c][:].rearrange("p (g i) t -> p g t i", i=4),
-                z_planes[:, c, :, :].rearrange("p t (g i) -> p g t i", i=4),
+                z_grouped[c][:].rearrange("p v t -> p (v t)").bitcast(F32).rearrange("p (v u) -> p v u", u=2),
+                pairs[c][:].rearrange("p u v e -> p (u v e)").bitcast(F32).rearrange("p (u v) -> p v u", u=2),
             )
 
         def quantise_z(c):
@@ -164,19 +213,18 @@ def tile_picked_unet_gelu_e_kernel(tc, xT, w1, w2, skip, offs, cell, out):
             nc.sync.dma_start(out_view[:, :, c * CELLS : (c + 1) * CELLS], result[c][:])
 
         on_scalar, on_vector = nc.scalar.copy, nc.vector.tensor_copy
-        add_last(0)
-        weave(on_scalar, 0)
-        add_last(3)
-        weave(on_scalar, 3)
-        add_last(1)
-        add_last(2)
-        weave(on_vector, 1)
-        quantise_z(0)
+        for b in range(N // P):
+            idle = psum.tile([P, S], F32, name="bank")
+            rows = slice(b * P, (b + 1) * P)
+            product(nc, idle[:], w2_words[:, rows], w2_scales[:, rows], x_words[:], x_scales[:])
+        for c in range(CHUNKS):
+            add_last(c)
+        for c in range(CHUNKS - 1):
+            weave(on_scalar, c)
+        weave(on_vector, CHUNKS - 1)
+        for c in (0, 3, 1, 2):
+            quantise_z(c)
         finish(0, [on_scalar, on_scalar])
-        quantise_z(1)
-        finish(1, [on_scalar, on_scalar])
-        weave(on_vector, 2)
-        quantise_z(3)
         finish(3, [on_scalar, on_vector])
-        quantise_z(2)
+        finish(1, [on_scalar, on_vector])
         finish(2, [on_scalar, on_vector])

from contextlib import ExitStack

import concourse.mybir as mybir
from concourse.masks import make_identity

K, T, S, H, N, U = 512, 2048, 512, 512, 256, 1024
FLOPS = 2 * K * H * S + 2 * H * N * U

F32 = mybir.dt.float32
BF16 = mybir.dt.bfloat16
U32 = mybir.dt.uint32
U16 = mybir.dt.uint16
U8 = mybir.dt.uint8
FP8X4 = mybir.dt.float8_e4m3fn_x4
ADD = mybir.AluOpType.add
GELU = mybir.ActivationFunctionType.Gelu_apprx_tanh

P = 128
PACK = 4
HALF = S // 2
LANES = 16
CELLS = 256
CHUNKS = U // CELLS
W1_HALF = H // 2
M_HALF = W1_HALF // PACK
ORDER = (0, 2, 3, 1)
BLOCKS = CELLS // P


def quantise(nc, words, scales, grouped):
    nc.vector.quantize_mx(out=words.bitcast(FP8X4), scales=scales, in_=grouped)


def product(nc, bank, w_words, w_scales, a_words, a_scales):
    nc.tensor.matmul_mx(
        out=bank,
        lhsT=w_words.bitcast(FP8X4),
        lhsT_scale=w_scales,
        rhs=a_words.bitcast(FP8X4),
        rhs_scale=a_scales,
        start=True,
        stop=True,
    )


def tile_picked_unet_gelu_e_kernel(tc, xT, w1, w2, skip, offs, cell, out):
    nc = tc.nc
    with ExitStack() as ctx:
        lists = ctx.enter_context(tc.tile_pool(name="lists", bufs=1))
        keep = ctx.enter_context(tc.tile_pool(name="keep", bufs=1))
        psum = ctx.enter_context(tc.psum_pool(name="psum", bufs=8))

        offs_sb = lists.tile([P, S // LANES], U16, name="offs_sb")
        cell_sb = lists.tile([P, S // LANES], U16, name="cell_sb")
        x_rows = [keep.tile([P, T], F32, name=f"x_rows{j}") for j in range(PACK)]
        w1_raw = [keep.tile([P, PACK, W1_HALF], F32, name=f"w1_raw{u}") for u in range(2)]
        w2_raw = keep.tile([P, PACK, N], F32, name="w2_raw")
        skip_rows = [keep.tile([P, U], F32, name=f"skip_rows{t}") for t in range(PACK)]

        x_view = xT.rearrange("(p j) c -> p j c", j=PACK)
        w1_view = w1.rearrange("(p j) c -> p j c", j=PACK)
        skip_view = skip.rearrange("(p t) v -> p t v", t=PACK)
        nc.sync.dma_start(offs_sb[:], offs)
        for j in range(PACK):
            nc.sync.dma_start(x_rows[j][:], x_view[:, j, :])
        for u in range(2):
            nc.sync.dma_start(w1_raw[u][:], w1_view[:, :, u * W1_HALF : (u + 1) * W1_HALF])
        nc.sync.dma_start(cell_sb[:], cell)
        nc.sync.dma_start(skip_rows[ORDER[0]][:], skip_view[:, ORDER[0], :])
        nc.sync.dma_start(w2_raw[:], w2.rearrange("(p j) c -> p j c", j=PACK))
        for t in ORDER[1:]:
            nc.sync.dma_start(skip_rows[t][:], skip_view[:, t, :])

        up = [keep.tile([P, U], F32, name=f"up{t}") for t in range(PACK)]
        for t in range(PACK):
            nc.vector.memset(up[t][:], 0.0)
        warm_in = keep.tile([P, 8], F32, name="warm_in")
        warm_out = keep.tile([P, 8], F32, name="warm_out")
        nc.vector.memset(warm_in[:], 0.0)
        nc.scalar.activation(warm_out[:], warm_in[:], GELU)

        x_grouped = keep.tile([P, S, PACK], BF16, name="x_grouped", align_bytes=64)
        x_words = keep.tile([P, S], U32, name="x_words", align_bytes=64)
        x_scales = keep.tile([P, S], U8, name="x_scales", align_bytes=64)
        halves = [slice(h * HALF, (h + 1) * HALF) for h in range(2)]
        list_halves = [slice(h * HALF // LANES, (h + 1) * HALF // LANES) for h in range(2)]
        for j in range(PACK - 1):
            nc.vector.tensor_copy(x_grouped[:, :, j], x_rows[j][:].indirect(offs_sb[:]))
        for h in range(2):
            nc.vector.tensor_copy(x_grouped[:, halves[h], PACK - 1], x_rows[PACK - 1][:].indirect(offs_sb[:, list_halves[h]]))
        for h in range(2):
            quantise(nc, x_words[:, halves[h]], x_scales[:, halves[h]], x_grouped[:, halves[h], :].rearrange("p s j -> p (s j)"))

        w1_first = keep.tile([P, P, PACK], BF16, name="w1_first", align_bytes=64)
        w1_rest = keep.tile([P, PACK - 1, P, PACK], BF16, name="w1_rest", align_bytes=64)
        w1_words = [keep.tile([P, P], U32, name=f"w1_words{t}", align_bytes=64) for t in range(PACK)]
        w1_scales = [keep.tile([P, P], U8, name=f"w1_scales{t}", align_bytes=64) for t in range(PACK)]

        def deal_w1(copy, u, first):
            dealt = w1_raw[u][:].rearrange("p j (m t) -> p m j t", t=PACK)
            ms = slice(u * M_HALF, (u + 1) * M_HALF)
            if first:
                copy(w1_first[:, ms, :], dealt[:, :, :, 0])
            else:
                copy(w1_rest[:, :, ms, :].rearrange("p t m j -> p m j t"), dealt[:, :, :, 1:PACK])

        deal_w1(nc.scalar.copy, 0, True)
        deal_w1(nc.scalar.copy, 0, False)
        deal_w1(nc.vector.tensor_copy, 1, True)
        quantise(nc, w1_words[0][:], w1_scales[0][:], w1_first[:].rearrange("p m j -> p (m j)"))
        deal_w1(nc.vector.tensor_copy, 1, False)
        for t in ORDER[1:]:
            quantise(nc, w1_words[t][:], w1_scales[t][:], w1_rest[:, t - 1, :, :].rearrange("p m j -> p (m j)"))

        eye32 = keep.tile([P, P], F32, name="eye32")
        eye16 = keep.tile([P, P], BF16, name="eye16")
        make_identity(nc, eye32[:])
        make_identity(nc, eye16[:])

        first, second, third, last = ORDER
        whole, whole_list = slice(0, S), slice(0, S // LANES)
        pieces = [
            (first, halves[0], list_halves[0]),
            (second, halves[0], list_halves[0]),
            (first, halves[1], list_halves[1]),
            (second, halves[1], list_halves[1]),
            (third, whole, whole_list),
            (last, whole, whole_list),
        ]
        for n, (t, entries, columns) in enumerate(pieces):
            width = entries.stop - entries.start
            bank = psum.tile([P, S], F32, name="bank")
            product(nc, bank[:, 0:width], w1_words[t][:], w1_scales[t][:], x_words[:, entries], x_scales[:, entries])
            hidden = keep.tile([P, width], F32, name=f"hidden{n}")
            nc.scalar.activation(hidden[:], bank[:, 0:width], GELU)
            nc.vector.tensor_copy(up[t][:].indirect(cell_sb[:, columns]), hidden[:])

        w2_grouped = keep.tile([P, N, PACK], BF16, name="w2_grouped", align_bytes=64)
        w2_words = keep.tile([P, N], U32, name="w2_words", align_bytes=64)
        w2_scales = keep.tile([P, N], U8, name="w2_scales", align_bytes=64)
        nc.scalar.copy(
            w2_grouped[:].rearrange("p (c i) j -> p c j i", i=4),
            w2_raw[:].rearrange("p j (c i) -> p c j i", i=4),
        )
        quantise(nc, w2_words[:], w2_scales[:], w2_grouped[:].rearrange("p m j -> p (m j)"))

        def summed_and_turned(t):
            sums = [psum.tile([P, 4, P], F32, name="bank") for g in range(2)]
            for source, start, stop in ((skip_rows[t], True, False), (up[t], False, True)):
                for block in range(U // P):
                    g, q = divmod(block, 4)
                    nc.tensor.matmul(
                        sums[g][:, q, :],
                        source[:, block * P : (block + 1) * P],
                        eye32[:],
                        start=start and q == 0,
                        stop=stop and q == 3,
                        is_transpose=True,
                    )
            return sums

        pairs = [keep.tile([P, 2, CELLS, 2], BF16, name=f"pairs{c}") for c in range(CHUNKS)]

        lone_sums = summed_and_turned(first)
        lone_back = psum.tile([P, U], BF16, name="bank")
        for g in range(2):
            lone_turned = keep.tile([P, 4, P], BF16, name=f"lone_turned{g}")
            nc.scalar.copy(lone_turned[:], lone_sums[g][:])
            for q in range(4):
                block = 4 * g + q
                nc.tensor.transpose(lone_back[:, block * P : (block + 1) * P], lone_turned[:, q, :], eye16[:])
        for c in range(CHUNKS):
            nc.scalar.copy(pairs[c][:, 0, :, :], lone_back[:, c * CELLS : (c + 1) * CELLS].unsqueeze(2).to_broadcast([P, CELLS, 2]))

        pair_turned = [keep.tile([P, 4 * P, 2], BF16, name=f"pair_turned{g}") for g in range(2)]
        for e, t in enumerate((second, third)):
            sums = summed_and_turned(t)
            for g in range(2):
                nc.scalar.copy(pair_turned[g][:, :, e], sums[g][:].rearrange("p q m -> p (q m)"))
        for c in range(CHUNKS):
            g, place = divmod(c * CELLS, 4 * P)
            words = pair_turned[g][:].rearrange("p w e -> p (w e)").bitcast(F32)
            pair_back = psum.tile([P, CELLS], F32, name="bank")
            for q in range(BLOCKS):
                nc.tensor.transpose(pair_back[:, q * P : (q + 1) * P], words[:, place + q * P : place + (q + 1) * P], eye32[:])
            nc.scalar.copy(pairs[c][:, 1, :, :].rearrange("p v e -> p (v e)").bitcast(F32), pair_back[:])

        z_grouped = [keep.tile([P, CELLS, PACK], BF16, name=f"z_grouped{c}", align_bytes=64) for c in range(CHUNKS)]
        z_words = [keep.tile([P, CELLS], U32, name=f"z_words{c}", align_bytes=64) for c in range(CHUNKS)]
        z_scales = [keep.tile([P, CELLS], U8, name=f"z_scales{c}", align_bytes=64) for c in range(CHUNKS)]
        result = [keep.tile([P, N // P, CELLS], F32, name=f"result{c}") for c in range(CHUNKS)]
        out_view = out.rearrange("(b p) v -> p b v", p=P)

        def add_last(c):
            cells = slice(c * CELLS, (c + 1) * CELLS)
            nc.vector.tensor_tensor(pairs[c][:, 0, :, 1], up[last][:, cells], skip_rows[last][:, cells], ADD)

        def weave(copy, c):
            copy(
                z_grouped[c][:].rearrange("p v t -> p (v t)").bitcast(F32).rearrange("p (v u) -> p v u", u=2),
                pairs[c][:].rearrange("p u v e -> p (u v e)").bitcast(F32).rearrange("p (u v) -> p v u", u=2),
            )

        def quantise_z(c):
            quantise(nc, z_words[c][:], z_scales[c][:], z_grouped[c][:].rearrange("p v t -> p (v t)"))

        def finish(c, copies):
            for b in range(N // P):
                bank = psum.tile([P, S], F32, name="bank")
                rows = slice(b * P, (b + 1) * P)
                product(nc, bank[:, 0:CELLS], w2_words[:, rows], w2_scales[:, rows], z_words[c][:], z_scales[c][:])
                copies[b](result[c][:, b, :], bank[:, 0:CELLS])
            nc.sync.dma_start(out_view[:, :, c * CELLS : (c + 1) * CELLS], result[c][:])

        on_scalar, on_vector = nc.scalar.copy, nc.vector.tensor_copy
        for b in range(N // P):
            idle = psum.tile([P, S], F32, name="bank")
            rows = slice(b * P, (b + 1) * P)
            product(nc, idle[:], w2_words[:, rows], w2_scales[:, rows], x_words[:], x_scales[:])
        for c in range(CHUNKS):
            add_last(c)
        for c in range(CHUNKS - 1):
            weave(on_scalar, c)
        weave(on_vector, CHUNKS - 1)
        for c in (0, 3, 1, 2):
            quantise_z(c)
        finish(0, [on_scalar, on_scalar])
        finish(3, [on_scalar, on_vector])
        finish(1, [on_scalar, on_vector])
        finish(2, [on_scalar, on_vector])
